import numpy as np
import ml_dtypes


def mxq(x, axis, fmt="e4m3"):
    dtype, down = {"e4m3": (ml_dtypes.float8_e4m3fn, 7), "e5m2": (ml_dtypes.float8_e5m2, 14)}[fmt]
    v = np.moveaxis(np.asarray(x, np.float32).astype(ml_dtypes.bfloat16).astype(np.float64), axis, -1)
    blocks = v.reshape(v.shape[:-1] + (-1, 32))
    amax = np.abs(blocks).max(-1, keepdims=True)
    byte = np.maximum(np.where(amax > 0, np.frexp(amax)[1] - 1 + 127, 0) - down, 1)
    scale = np.exp2(byte - 127.0)
    codes = (blocks / scale).astype(np.float32).astype(dtype).astype(np.float64)
    return np.moveaxis((codes * scale).reshape(v.shape), -1, axis)


WIDE = False


def mx_kscale(k):
    if not WIDE:
        return np.ones(k)
    levels = np.array([10, -10, 5, -5, 0])
    if k % 512:
        return np.exp2(np.random.permutation(np.resize(levels, k // 32))).repeat(32)
    a = np.empty((k // 512, 16))
    for p in range(k // 512):
        a[p, :8] = np.random.permutation(np.resize(levels, 8))
        for g in range(8):
            far = levels[np.abs(levels - a[p, g]) >= 10]
            a[p, g + 8] = far[np.random.randint(len(far))]
    return np.exp2(a.ravel()).repeat(32)


def f64(x):
    return np.asarray(x).astype(np.float64)


def striped(idx):
    return np.tile(idx.reshape(-1, 16).T, (8, 1)).astype(np.uint16)


def unstriped(offs):
    return offs[:16].T.reshape(-1).astype(np.int64)


def striped8(idx):
    return np.concatenate([x.reshape(-1, 16).T for x in idx]).astype(np.uint16)


def runs(offs, k):
    lists = np.stack([offs[16 * r : 16 * r + 16].T.reshape(-1) for r in range(8)]).astype(np.int64)
    return lists[np.arange(k) % 512 // 64]


def pack_weight(w):
    k, n = w.shape
    w = f64(np.asarray(w, np.float32).astype(ml_dtypes.bfloat16)).reshape(k // 32, 32, n)
    amax = np.abs(w).max(1)
    byte = np.clip(np.where(amax > 0, np.frexp(amax)[1] - 1 + 127 - 7, 1), 1, 254)
    scaled = (w * np.exp2(127.0 - byte)[:, None, :]).reshape(k, n).astype(np.float32)
    words = np.ascontiguousarray(scaled.reshape(k // 512, 128, 4, n).transpose(0, 1, 3, 2)).astype(ml_dtypes.float8_e4m3fn).view(np.uint8)
    return words, np.ascontiguousarray(byte.astype(np.uint8).reshape(k // 512, 16, n))


def unpack_weight(words, scales):
    g, p, n, _ = words.shape
    vals = np.ascontiguousarray(words).view(ml_dtypes.float8_e4m3fn).astype(np.float64) * np.repeat(np.exp2(scales.astype(np.float64) - 127.0), 8, axis=1)[..., None]
    return vals.transpose(0, 1, 3, 2).reshape(g * 512, n)


E2M1 = np.array([0.0, 0.5, 1.0, 1.5, 2.0, 3.0, 4.0, 6.0, -0.0, -0.5, -1.0, -1.5, -2.0, -3.0, -4.0, -6.0])


def pack_fp4(w):
    k, n = w.shape
    w = f64(np.asarray(w, np.float32).astype(ml_dtypes.bfloat16)).reshape(k // 32, 32, n)
    amax = np.abs(w).max(1)
    mant, ex = np.frexp(amax / 6.0)
    byte = np.clip(np.where(amax > 0, np.where(mant > 0.5, ex, ex - 1) + 127, 1), 1, 254)
    scaled = (w * np.exp2(127.0 - byte)[:, None, :]).reshape(k, n).astype(np.float32)
    c = np.ascontiguousarray(scaled.reshape(k // 512, 128, 4, n).transpose(0, 1, 3, 2)).astype(ml_dtypes.float4_e2m1fn).view(np.uint8) & 0xF
    words = (c[..., 0::2] | (c[..., 1::2] << 4)).reshape(k // 512, 128, 2 * n)
    return np.ascontiguousarray(words), np.ascontiguousarray(byte.astype(np.uint8).reshape(k // 512, 16, n))


def unpack_fp4(words, scales):
    g, _, n = scales.shape
    words = np.ascontiguousarray(words).reshape(g, 128, n, 2)
    nib = np.empty((g, 128, n, 4), np.uint8)
    nib[..., 0::2] = words & 0xF
    nib[..., 1::2] = words >> 4
    vals = E2M1[nib] * np.repeat(np.exp2(scales.astype(np.float64) - 127.0), 8, axis=1)[..., None]
    return vals.transpose(0, 1, 3, 2).reshape(g * 512, n)


def planes(y):
    n, m = y.shape
    v = y.astype(np.float32).astype(ml_dtypes.bfloat16).astype(np.float64).reshape(n // 32, 32, m)
    top = np.abs(v).max(1)
    byte = np.clip(np.where(top > 0, np.frexp(top)[1] - 1 + 127 - 7, 1), 1, 254)
    codes = (v * np.exp2(127.0 - byte)[:, None, :]).reshape(n, m).astype(np.float32).astype(ml_dtypes.float8_e4m3fn).view(np.uint8)
    words = codes.reshape(n // 512, 128, 4, m).transpose(0, 1, 3, 2)
    return np.ascontiguousarray(words), np.ascontiguousarray(byte.astype(np.uint8).reshape(n // 512, 16, m))


K, T, S, N, G, H = 512, 2048, 512, 512, 2048, 512


def setup_inputs():
    n = np.random.standard_normal
    s = mx_kscale(K)[:, None]
    u = mx_kscale(H)
    packed_xT = pack_weight(n((K, T)) * s)
    packed_dT = pack_weight(n((K, G)) / s)
    packed_w1 = pack_fp4(n((H, N)) / np.sqrt(H) / u[:, None])
    return {
        "x_words": packed_xT[0],
        "x_scales": packed_xT[1],
        "d_words": packed_dT[0],
        "d_scales": packed_dT[1],
        "gn": (np.random.uniform(0.5, 1.5, (H, 1)) * u[:, None]).astype(np.float32),
        "w1_words": packed_w1[0],
        "w1_scales": packed_w1[1],
        "offs": striped(np.random.permutation(T)[:S]),
        "kidx": striped8(np.random.randint(0, G, (8, H))),
        "n1": striped8(np.stack([np.random.permutation(S) for _ in range(8)])),
        "n2": striped8(np.stack([np.random.permutation(S) for _ in range(8)])),
    }


def reference(x_words, x_scales, d_words, d_scales, gn, w1_words, w1_scales, offs, kidx, n1, n2):
    d_kidx = unpack_weight(d_words, d_scales)[np.arange(K)[:, None], runs(kidx, K)]
    xq = unpack_weight(x_words, x_scales)[:, unstriped(offs)]
    s = 0.0625 * (d_kidx.T @ xq)
    z = f64(gn) * ((s[np.arange(H)[:, None], runs(n1, H)]) * (np.tanh(s - (s[np.arange(H)[:, None], runs(n2, H)]))))
    out_0 = unpack_fp4(w1_words, w1_scales).T @ mxq(z, 0, "e4m3")
    return (out_0,) + planes(out_0)

@@ -1,0 +1,274 @@
+from contextlib import ExitStack
+
+import concourse.mybir as mybir
+
+F32 = mybir.dt.float32
+BF16 = mybir.dt.bfloat16
+I32 = mybir.dt.int32
+U32 = mybir.dt.uint32
+U16 = mybir.dt.uint16
+U8 = mybir.dt.uint8
+FP8X4 = mybir.dt.float8_e4m3fn_x4
+FP4X4 = mybir.dt.float4_e2m1fn_x4
+ACT = mybir.ActivationFunctionType
+ALU = mybir.AluOpType
+
+P = 128
+PACK = 4
+TABLE = 2048
+S = 512
+HALF = 256
+CHUNKS = ((0, 256), (256, 128), (384, 128))
+TINY = 2.0**-126
+FLOPS = 2 * 2 * 512 * 512 * 512
+
+
+def tile_picked_scoretan_none_po_kernel(
+    tc, x_words, x_scales, d_words, d_scales, gn, w1_words, w1_scales, offs, kidx, n1, n2, out_0, out_1, out_2
+):
+    nc = tc.nc
+    with ExitStack() as ctx:
+        sb = ctx.enter_context(tc.tile_pool(name="sb", bufs=1))
+        ps = ctx.enter_context(tc.psum_pool(name="ps", bufs=1))
+
+        def tile(shape, dtype, name, tag=None):
+            return sb.tile(shape, dtype, name=name, tag=tag or name, align_bytes=64)
+
+        kidx_t = tile([P, S // 16], U16, "kidx_t")
+        offs_t = tile([P, S // 16], U16, "offs_t")
+        n1_t = tile([P, S // 16], U16, "n1_t")
+        n2_t = tile([P, S // 16], U16, "n2_t")
+        dw = tile([P, TABLE], U32, "dw")
+        ds = tile([P, TABLE], U8, "ds")
+        xs = tile([P, TABLE], U8, "xs")
+
+        warm = tile([P, 2], F32, "warm")
+        nc.vector.memset(warm[:, 0:1], 0.0)
+        nc.scalar.activation(warm[:, 1:2], warm[:, 0:1], ACT.Tanh)
+        nc.gpsimd.memset(xs[:].bitcast(I32), 0)
+        gn_t = tile([P, PACK], F32, "gn_t")
+
+        nc.sync.dma_start(kidx_t[:], kidx)
+        nc.sync.dma_start(out=ds[:].bitcast(I32), in_=d_scales[0].bitcast(I32).unsqueeze(1).to_broadcast([16, 8, TABLE // 4]))
+        nc.sync.dma_start(out=gn_t[:], in_=gn.rearrange("(p t) o -> p (t o)", t=PACK))
+        nc.sync.dma_start(offs_t[:], offs)
+        nc.sync.dma_start(n2_t[:], n2)
+        nc.sync.dma_start(out=dw[:].bitcast(I32), in_=d_words[0].rearrange("p n t -> p (n t)").bitcast(I32))
+        nc.sync.dma_start(n1_t[:], n1)
+        for q, queue in enumerate((nc.sync, nc.sync, nc.gpsimd, nc.gpsimd)):
+            queue.dma_start(out=xs[32 * q : 32 * q + 4, :].bitcast(I32), in_=x_scales[0, 4 * q : 4 * q + 4, :].bitcast(I32))
+        xw = tile([P, TABLE], U32, "xw", tag="warm")
+        nc.sync.dma_start(out=xw[:].bitcast(I32), in_=x_words[0].rearrange("p n t -> p (n t)").bitcast(I32))
+
+        def deal(dst, src, run):
+            nc.vector.tensor_copy(
+                out=dst.rearrange("p (t c i) -> p c t i", t=PACK, i=run),
+                in_=src.rearrange("p (c i t) -> p c t i", t=PACK, i=run),
+            )
+
+        ds_g = tile([P, S], U8, "ds_g")
+        nc.vector.tensor_copy(ds_g[:], ds[:].indirect(kidx_t[:]))
+        ds_d = tile([P, S], U8, "ds_d")
+        deal(ds_d[:], ds_g[:], 16)
+        for r in range(1, 4):
+            nc.scalar.dma_start(out=ds_d[r:P:32, :].bitcast(I32), in_=ds_d[8 * r : P : 32, :].bitcast(I32))
+        w1w = tile([P, 2 * S], U8, "w1w", tag="ds_g")
+        nc.scalar.dma_start(out=w1w[:].bitcast(I32), in_=w1_words[0].bitcast(I32))
+        xs_g = tile([P, S], U8, "xs_g")
+        nc.vector.tensor_copy(xs_g[:], xs[:].indirect(offs_t[:]))
+        w1s = tile([P, S], U8, "w1s", tag="xs")
+        nc.gpsimd.memset(w1s[:].bitcast(I32), 0)
+        for q in range(4):
+            nc.sync.dma_start(out=w1s[32 * q : 32 * q + 4, :].bitcast(I32), in_=w1_scales[0, 4 * q : 4 * q + 4, :].bitcast(I32))
+        dw_g = tile([P, S], U32, "dw_g")
+        nc.vector.tensor_copy(dw_g[:], dw[:].indirect(kidx_t[:]))
+        dw_d = tile([P, S], U32, "dw_d")
+        deal(dw_d[:].bitcast(I32), dw_g[:].bitcast(I32), 4)
+        xw_g = tile([P, S], U32, "xw_g")
+        for h in range(2):
+            nc.vector.tensor_copy(xw_g[:, h * HALF : (h + 1) * HALF], xw[:].indirect(offs_t[:, 16 * h : 16 * h + 16]))
+
+        gs = tile([P, PACK], F32, "gs")
+        nc.gpsimd.tensor_scalar(gs[:], gn_t[:], 0.0625, 0.0, ALU.mult, ALU.add)
+        above = tile([P, PACK], F32, "above")
+        nc.gpsimd.tensor_scalar(above[:], gn_t[:], -TINY, None, ALU.is_gt)
+        below = tile([P, PACK], F32, "below")
+        nc.gpsimd.tensor_scalar(below[:], gn_t[:], TINY, None, ALU.is_lt)
+        nc.gpsimd.tensor_tensor(above[:], above[:], below[:], ALU.mult)
+        nc.gpsimd.tensor_tensor(below[:], above[:], gn_t[:], ALU.add)
+        nc.gpsimd.tensor_scalar(above[:], below[:], -1.0, 0.0, ALU.mult, ALU.add)
+
+        def mm1(acc, t, c0, n):
+            nc.tensor.matmul_mx(
+                out=acc,
+                lhsT=dw_d[:, t * P : (t + 1) * P].bitcast(FP8X4),
+                lhsT_scale=ds_d[:, t * P : (t + 1) * P],
+                rhs=xw_g[:, c0 : c0 + n].bitcast(FP8X4),
+                rhs_scale=xs_g[:, c0 : c0 + n],
+                start=True,
+                stop=True,
+            )
+
+        raw = {}
+        for h in range(2):
+            bank = ps.tile([P, HALF], F32, name="raw0%d" % h)
+            mm1(bank[:], 0, h * HALF, HALF)
+            raw[0, h] = bank[:]
+        for t in range(1, PACK):
+            bank = ps.tile([P, S], F32, name="raw%d" % t)
+            mm1(bank[:], t, 0, S)
+            raw[t] = bank
+
+        w1w_d = tile([P, 2 * S], U8, "w1w_d", tag="warm")
+        nc.vector.tensor_copy(
+            out=w1w_d[:].rearrange("p (t c i b) -> p c t i b", t=PACK, i=8, b=2),
+            in_=w1w[:].rearrange("p (c i t b) -> p c t i b", t=PACK, i=8, b=2),
+        )
+
+        rg = tile([P, PACK], F32, "rg", tag="ds_g")
+        nc.vector.reciprocal(rg[:], above[:])
+
+        win = [tile([P, S], F32, "win_%d" % t) for t in range(PACK)]
+        plain = [[tile([P, HALF], F32, "plain_%d_%d" % (t, h)) for h in range(2)] for t in range(PACK)]
+        diff = [tile([P, S], F32, "diff_%d" % t) for t in range(PACK)]
+        tanh = [tile([P, S], F32, "tanh_%d" % t) for t in range(PACK)]
+        zf = {}
+        oq = tile([P, S], U32, "oq")
+        osc = tile([P, S], U8, "osc")
+
+        def half(h):
+            return slice(h * HALF, (h + 1) * HALF)
+
+        def raw_half(t, h):
+            return raw[0, h] if t == 0 else raw[t][:, half(h)]
+
+        def scaled(dst, src, t):
+            nc.scalar.activation(dst, src, ACT.Copy, scale=gs[:, t : t + 1])
+
+        def window(t):
+            scaled(win[t][:], raw[t][:], t)
+
+        def own(t, h):
+            scaled(plain[t][h][:], raw_half(t, h), t)
+
+        def sub(t, h):
+            nc.vector.tensor_tensor(diff[t][:, half(h)], win[t][:].indirect(n2_t[:, 16 * h : 16 * h + 16]), plain[t][h][:], ALU.subtract)
+
+        def th(t, h):
+            nc.scalar.activation(tanh[t][:, half(h)], diff[t][:, half(h)], ACT.Tanh, scale=rg[:, t : t + 1])
+
+        def mul(t, ch):
+            c0, n = CHUNKS[ch]
+            if t == 0:
+                zf[ch] = tile([P, PACK, n], F32, "zf_%d" % ch, tag="zb_0" if ch == 1 else None)
+            nc.vector.tensor_tensor(
+                zf[ch][:, t, :], win[t][:].indirect(n1_t[:, c0 // 16 : (c0 + n) // 16]), tanh[t][:, c0 : c0 + n], ALU.mult
+            )
+
+        def weave_views(dst, src):
+            return (
+                dst[:].rearrange("p (c i t) -> p c t i", t=PACK, i=4),
+                src[:].rearrange("p t (c i) -> p c t i", i=4),
+            )
+
+        zb, zq, zs, acc, of, ob = {}, {}, {}, {}, {}, {}
+
+        def weave_z(ch, eng):
+            n = CHUNKS[ch][1]
+            zb[ch] = tile([P, PACK * n], BF16, "zb_%d" % ch)
+            d, s = weave_views(zb[ch], zf[ch])
+            if eng == "s":
+                nc.scalar.copy(d, s)
+            else:
+                nc.vector.tensor_copy(d, s)
+
+        def quant_z(ch):
+            n = CHUNKS[ch][1]
+            zq[ch] = tile([P, n], U32, "zq_%d" % ch)
+            zs[ch] = tile([P, n], U8, "zs_%d" % ch)
+            nc.vector.quantize_mx(out=zq[ch][:].bitcast(FP8X4), scales=zs[ch][:], in_=zb[ch][:])
+
+        def mm2(ch):
+            c0, n = CHUNKS[ch]
+            per = S // n
+            of[ch] = tile([P, PACK, n], F32, "of_%d" % ch)
+            for b in range(PACK // per):
+                bank = ps.tile([P, per, n], F32, name="acc_%d_%d" % (ch, b), tag="acc", bufs=3)
+                for u in range(per):
+                    t = b * per + u
+                    nc.tensor.matmul_mx(
+                        out=bank[:, u, :],
+                        lhsT=w1w_d[:, 2 * t * P : 2 * (t + 1) * P].bitcast(FP4X4),
+                        lhsT_scale=w1s_d[:, t * P : (t + 1) * P],
+                        rhs=zq[ch][:].bitcast(FP8X4),
+                        rhs_scale=zs[ch][:],
+                        start=True,
+                        stop=True,
+                    )
+                nc.scalar.copy(of[ch][:, b * per : (b + 1) * per, :], bank[:])
+            nc.sync.dma_start(out=out_0.rearrange("(p t) j -> p t j", t=PACK)[:, :, c0 : c0 + n], in_=of[ch][:])
+
+        def weave_o(ch, eng):
+            n = CHUNKS[ch][1]
+            ob[ch] = tile([P, PACK * n], BF16, "ob_%d" % ch)
+            d, s = weave_views(ob[ch], of[ch])
+            if eng == "s":
+                nc.scalar.copy(d, s)
+            else:
+                nc.vector.tensor_copy(d, s)
+
+        def quant_o(ch):
+            c0, n = CHUNKS[ch]
+            nc.vector.quantize_mx(out=oq[:, c0 : c0 + n].bitcast(FP8X4), scales=osc[:, c0 : c0 + n], in_=ob[ch][:])
+            nc.sync.dma_start(
+                out=out_1[0].rearrange("p n t -> p (n t)").bitcast(I32)[:, c0 : c0 + n],
+                in_=oq[:, c0 : c0 + n].bitcast(I32),
+            )
+
+        scaled(win[0][:, half(0)], raw[0, 0], 0)
+        own(0, 0)
+        scaled(win[0][:, half(1)], raw[0, 1], 0)
+        sub(0, 0)
+        for t in range(1, PACK):
+            window(t)
+            own(t, 0)
+            sub(t, 0)
+            th(t - 1, 0)
+            mul(t - 1, 0)
+        own(0, 1)
+        sub(0, 1)
+        th(PACK - 1, 0)
+        mul(PACK - 1, 0)
+        w1s_d = tile([P, S], U8, "w1s_d", tag="plain_3_0")
+        deal(w1s_d[:], w1s[:], 16)
+        own(1, 1)
+        sub(1, 1)
+        weave_z(0, "s")
+        own(2, 1)
+        sub(2, 1)
+        quant_z(0)
+        own(3, 1)
+        sub(3, 1)
+        for t in range(PACK):
+            th(t, 1)
+            mul(t, 1)
+        mm2(0)
+        weave_z(1, "s")
+        mul(0, 2)
+        mul(1, 2)
+        quant_z(1)
+        weave_o(0, "s")
+        mul(2, 2)
+        mul(3, 2)
+        mm2(1)
+        weave_z(2, "v")
+        quant_z(2)
+        mm2(2)
+        quant_o(0)
+        weave_o(1, "v")
+        quant_o(1)
+        weave_o(2, "v")
+        quant_o(2)
+        for q in range(4):
+            queue = nc.scalar if q % 2 else nc.sync
+            queue.dma_start(out=out_2[0, 4 * q : 4 * q + 4, :].bitcast(I32), in_=osc[32 * q : 32 * q + 4, :].bitcast(I32))

@@ -44,20 +44,18 @@ def tile_picked_scoretan_none_po_kernel(
 
         warm = tile([P, 2], F32, "warm")
         nc.vector.memset(warm[:, 0:1], 0.0)
-        nc.scalar.activation(warm[:, 1:2], warm[:, 0:1], ACT.Tanh)
-        nc.gpsimd.memset(xs[:].bitcast(I32), 0)
         gn_t = tile([P, PACK], F32, "gn_t")
 
         nc.sync.dma_start(kidx_t[:], kidx)
         nc.sync.dma_start(out=ds[:].bitcast(I32), in_=d_scales[0].bitcast(I32).unsqueeze(1).to_broadcast([16, 8, TABLE // 4]))
-        nc.sync.dma_start(out=gn_t[:], in_=gn.rearrange("(p t) o -> p (t o)", t=PACK))
+        nc.scalar.dma_start(out=gn_t[:], in_=gn.rearrange("(p t) o -> p (t o)", t=PACK))
+        nc.scalar.activation(warm[:, 1:2], warm[:, 0:1], ACT.Tanh)
         nc.sync.dma_start(offs_t[:], offs)
-        nc.sync.dma_start(n2_t[:], n2)
+        nc.sync.dma_start(out=xs[:].bitcast(I32), in_=x_scales[0].bitcast(I32).unsqueeze(1).to_broadcast([16, 8, TABLE // 4]))
         nc.sync.dma_start(out=dw[:].bitcast(I32), in_=d_words[0].rearrange("p n t -> p (n t)").bitcast(I32))
+        nc.sync.dma_start(n2_t[:], n2)
         nc.sync.dma_start(n1_t[:], n1)
-        for q, queue in enumerate((nc.sync, nc.sync, nc.gpsimd, nc.gpsimd)):
-            queue.dma_start(out=xs[32 * q : 32 * q + 4, :].bitcast(I32), in_=x_scales[0, 4 * q : 4 * q + 4, :].bitcast(I32))
-        xw = tile([P, TABLE], U32, "xw", tag="warm")
+        xw = tile([P, TABLE], U32, "xw")
         nc.sync.dma_start(out=xw[:].bitcast(I32), in_=x_words[0].rearrange("p n t -> p (n t)").bitcast(I32))
 
         def deal(dst, src, run):
@@ -68,26 +66,19 @@ def tile_picked_scoretan_none_po_kernel(
 
         ds_g = tile([P, S], U8, "ds_g")
         nc.vector.tensor_copy(ds_g[:], ds[:].indirect(kidx_t[:]))
-        ds_d = tile([P, S], U8, "ds_d")
-        deal(ds_d[:], ds_g[:], 16)
-        for r in range(1, 4):
-            nc.scalar.dma_start(out=ds_d[r:P:32, :].bitcast(I32), in_=ds_d[8 * r : P : 32, :].bitcast(I32))
-        w1w = tile([P, 2 * S], U8, "w1w", tag="ds_g")
-        nc.scalar.dma_start(out=w1w[:].bitcast(I32), in_=w1_words[0].bitcast(I32))
         xs_g = tile([P, S], U8, "xs_g")
         nc.vector.tensor_copy(xs_g[:], xs[:].indirect(offs_t[:]))
-        w1s = tile([P, S], U8, "w1s", tag="xs")
-        nc.gpsimd.memset(w1s[:].bitcast(I32), 0)
-        for q in range(4):
-            nc.sync.dma_start(out=w1s[32 * q : 32 * q + 4, :].bitcast(I32), in_=w1_scales[0, 4 * q : 4 * q + 4, :].bitcast(I32))
-        dw_g = tile([P, S], U32, "dw_g")
+        sc = tile([P, 2 * S], U8, "sc")
+        deal(sc[:, 0:S], ds_g[:], 16)
+        nc.vector.tensor_copy(sc[:, S : 2 * S].bitcast(I32), xs_g[:].bitcast(I32))
+        for r in range(1, 4):
+            (nc.sync if r == 2 else nc.scalar).dma_start(out=sc[r:P:32, :].bitcast(I32), in_=sc[8 * r : P : 32, :].bitcast(I32))
+        w1w = tile([P, 2 * S], U8, "w1w", tag="xs_g")
+        nc.scalar.dma_start(out=w1w[:].bitcast(I32), in_=w1_words[0].bitcast(I32))
+        dw_g = tile([P, S], U32, "dw_g", tag="xs")
         nc.vector.tensor_copy(dw_g[:], dw[:].indirect(kidx_t[:]))
         dw_d = tile([P, S], U32, "dw_d")
         deal(dw_d[:].bitcast(I32), dw_g[:].bitcast(I32), 4)
-        xw_g = tile([P, S], U32, "xw_g")
-        for h in range(2):
-            nc.vector.tensor_copy(xw_g[:, h * HALF : (h + 1) * HALF], xw[:].indirect(offs_t[:, 16 * h : 16 * h + 16]))
-
         gs = tile([P, PACK], F32, "gs")
         nc.gpsimd.tensor_scalar(gs[:], gn_t[:], 0.0625, 0.0, ALU.mult, ALU.add)
         above = tile([P, PACK], F32, "above")
@@ -97,14 +88,23 @@ def tile_picked_scoretan_none_po_kernel(
         nc.gpsimd.tensor_tensor(above[:], above[:], below[:], ALU.mult)
         nc.gpsimd.tensor_tensor(below[:], above[:], gn_t[:], ALU.add)
         nc.gpsimd.tensor_scalar(above[:], below[:], -1.0, 0.0, ALU.mult, ALU.add)
+        rg = tile([P, PACK], F32, "rg", tag="dw")
+        nc.vector.reciprocal(rg[:], above[:])
+        w1s = tile([P, S], U8, "w1s", tag="xs")
+        nc.vector.memset(w1s[:].bitcast(I32), 0)
+        for q in range(4):
+            nc.sync.dma_start(out=w1s[32 * q : 32 * q + 4, :].bitcast(I32), in_=w1_scales[0, 4 * q : 4 * q + 4, :].bitcast(I32))
+        xw_g = tile([P, S], U32, "xw_g")
+        for h in range(2):
+            nc.vector.tensor_copy(xw_g[:, h * HALF : (h + 1) * HALF], xw[:].indirect(offs_t[:, 16 * h : 16 * h + 16]))
 
         def mm1(acc, t, c0, n):
             nc.tensor.matmul_mx(
                 out=acc,
                 lhsT=dw_d[:, t * P : (t + 1) * P].bitcast(FP8X4),
-                lhsT_scale=ds_d[:, t * P : (t + 1) * P],
+                lhsT_scale=sc[:, t * P : (t + 1) * P],
                 rhs=xw_g[:, c0 : c0 + n].bitcast(FP8X4),
-                rhs_scale=xs_g[:, c0 : c0 + n],
+                rhs_scale=sc[:, S + c0 : S + c0 + n],
                 start=True,
                 stop=True,
             )
@@ -119,18 +119,17 @@ def tile_picked_scoretan_none_po_kernel(
             mm1(bank[:], t, 0, S)
             raw[t] = bank
 
-        w1w_d = tile([P, 2 * S], U8, "w1w_d", tag="warm")
+        w1w_d = tile([P, 2 * S], U8, "w1w_d", tag="xw")
         nc.vector.tensor_copy(
             out=w1w_d[:].rearrange("p (t c i b) -> p c t i b", t=PACK, i=8, b=2),
             in_=w1w[:].rearrange("p (c i t b) -> p c t i b", t=PACK, i=8, b=2),
         )
 
-        rg = tile([P, PACK], F32, "rg", tag="ds_g")
-        nc.vector.reciprocal(rg[:], above[:])
 
         win = [tile([P, S], F32, "win_%d" % t) for t in range(PACK)]
-        plain = [[tile([P, HALF], F32, "plain_%d_%d" % (t, h)) for h in range(2)] for t in range(PACK)]
-        diff = [tile([P, S], F32, "diff_%d" % t) for t in range(PACK)]
+        plain = {(t, 0): tile([P, HALF], F32, "plain_%d" % t)[:] for t in range(PACK)}
+        plain[0, 1] = tile([P, HALF], F32, "plain_0_1")[:]
+        diff = [[tile([P, HALF], F32, "diff_%d_%d" % (t, h)) for h in range(2)] for t in range(PACK)]
         tanh = [tile([P, S], F32, "tanh_%d" % t) for t in range(PACK)]
         zf = {}
         oq = tile([P, S], U32, "oq")
@@ -149,18 +148,20 @@ def tile_picked_scoretan_none_po_kernel(
             scaled(win[t][:], raw[t][:], t)
 
         def own(t, h):
-            scaled(plain[t][h][:], raw_half(t, h), t)
+            scaled(plain[t, h], raw_half(t, h), t)
 
         def sub(t, h):
-            nc.vector.tensor_tensor(diff[t][:, half(h)], win[t][:].indirect(n2_t[:, 16 * h : 16 * h + 16]), plain[t][h][:], ALU.subtract)
+            nc.vector.tensor_tensor(diff[t][h][:], win[t][:].indirect(n2_t[:, 16 * h : 16 * h + 16]), plain[t, h], ALU.subtract)
 
-        def th(t, h):
-            nc.scalar.activation(tanh[t][:, half(h)], diff[t][:, half(h)], ACT.Tanh, scale=rg[:, t : t + 1])
+        def th(t, ch):
+            c0, n = CHUNKS[ch]
+            src = diff[t][c0 // HALF][:, c0 % HALF : c0 % HALF + n]
+            nc.scalar.activation(tanh[t][:, c0 : c0 + n], src, ACT.Tanh, scale=rg[:, t : t + 1])
 
         def mul(t, ch):
             c0, n = CHUNKS[ch]
             if t == 0:
-                zf[ch] = tile([P, PACK, n], F32, "zf_%d" % ch, tag="zb_0" if ch == 1 else None)
+                zf[ch] = tile([P, PACK, n], F32, "zf_%d" % ch)
             nc.vector.tensor_tensor(
                 zf[ch][:, t, :], win[t][:].indirect(n1_t[:, c0 // 16 : (c0 + n) // 16]), tanh[t][:, c0 : c0 + n], ALU.mult
             )
@@ -175,7 +176,7 @@ def tile_picked_scoretan_none_po_kernel(
 
         def weave_z(ch, eng):
             n = CHUNKS[ch][1]
-            zb[ch] = tile([P, PACK * n], BF16, "zb_%d" % ch)
+            zb[ch] = tile([P, PACK * n], BF16, "zb_%d" % ch, tag="zb_%d" % min(ch, 1))
             d, s = weave_views(zb[ch], zf[ch])
             if eng == "s":
                 nc.scalar.copy(d, s)
@@ -235,37 +236,34 @@ def tile_picked_scoretan_none_po_kernel(
             sub(t, 0)
             th(t - 1, 0)
             mul(t - 1, 0)
+            if t == 1:
+                w1s_d = tile([P, S], U8, "w1s_d", tag="diff_0_0")
+                deal(w1s_d[:], w1s[:], 16)
         own(0, 1)
         sub(0, 1)
         th(PACK - 1, 0)
         mul(PACK - 1, 0)
-        w1s_d = tile([P, S], U8, "w1s_d", tag="plain_3_0")
-        deal(w1s_d[:], w1s[:], 16)
-        own(1, 1)
-        sub(1, 1)
+        late = tile([P, PACK - 1, HALF], F32, "late", tag="diff_3_0")
+        for t in range(1, PACK):
+            plain[t, 1] = late[:, t - 1, :]
+            own(t, 1)
+            sub(t, 1)
         weave_z(0, "s")
-        own(2, 1)
-        sub(2, 1)
         quant_z(0)
-        own(3, 1)
-        sub(3, 1)
-        for t in range(PACK):
-            th(t, 1)
-            mul(t, 1)
-        mm2(0)
+        for ch in (1, 2):
+            for t in range(PACK):
+                th(t, ch)
+                mul(t, ch)
         weave_z(1, "s")
-        mul(0, 2)
-        mul(1, 2)
+        mm2(0)
         quant_z(1)
-        weave_o(0, "s")
-        mul(2, 2)
-        mul(3, 2)
         mm2(1)
         weave_z(2, "v")
         quant_z(2)
         mm2(2)
-        quant_o(0)
+        weave_o(0, "v")
         weave_o(1, "v")
+        quant_o(0)
         quant_o(1)
         weave_o(2, "v")
         quant_o(2)

@@ -42,19 +42,20 @@ def tile_picked_scoretan_none_po_kernel(
         ds = tile([P, TABLE], U8, "ds")
         xs = tile([P, TABLE], U8, "xs")
 
+        nc.gpsimd.memset(xs[:].bitcast(I32), 0)
         warm = tile([P, 2], F32, "warm")
         nc.vector.memset(warm[:, 0:1], 0.0)
         gn_t = tile([P, PACK], F32, "gn_t")
 
         nc.sync.dma_start(kidx_t[:], kidx)
         nc.sync.dma_start(out=ds[:].bitcast(I32), in_=d_scales[0].bitcast(I32).unsqueeze(1).to_broadcast([16, 8, TABLE // 4]))
-        nc.scalar.dma_start(out=gn_t[:], in_=gn.rearrange("(p t) o -> p (t o)", t=PACK))
+        nc.scalar.dma_start(out=xs[0:P:8, :].bitcast(I32), in_=x_scales[0].bitcast(I32))
         nc.scalar.activation(warm[:, 1:2], warm[:, 0:1], ACT.Tanh)
         nc.sync.dma_start(offs_t[:], offs)
-        nc.sync.dma_start(out=xs[:].bitcast(I32), in_=x_scales[0].bitcast(I32).unsqueeze(1).to_broadcast([16, 8, TABLE // 4]))
-        nc.sync.dma_start(out=dw[:].bitcast(I32), in_=d_words[0].rearrange("p n t -> p (n t)").bitcast(I32))
+        nc.sync.dma_start(out=gn_t[:], in_=gn.rearrange("(p t) o -> p (t o)", t=PACK))
         nc.sync.dma_start(n2_t[:], n2)
         nc.sync.dma_start(n1_t[:], n1)
+        nc.sync.dma_start(out=dw[:].bitcast(I32), in_=d_words[0].rearrange("p n t -> p (n t)").bitcast(I32))
         xw = tile([P, TABLE], U32, "xw")
         nc.sync.dma_start(out=xw[:].bitcast(I32), in_=x_words[0].rearrange("p n t -> p (n t)").bitcast(I32))
 
@@ -72,7 +73,7 @@ def tile_picked_scoretan_none_po_kernel(
         deal(sc[:, 0:S], ds_g[:], 16)
         nc.vector.tensor_copy(sc[:, S : 2 * S].bitcast(I32), xs_g[:].bitcast(I32))
         for r in range(1, 4):
-            (nc.sync if r == 2 else nc.scalar).dma_start(out=sc[r:P:32, :].bitcast(I32), in_=sc[8 * r : P : 32, :].bitcast(I32))
+            nc.scalar.dma_start(out=sc[r:P:32, :].bitcast(I32), in_=sc[8 * r : P : 32, :].bitcast(I32))
         w1w = tile([P, 2 * S], U8, "w1w", tag="xs_g")
         nc.scalar.dma_start(out=w1w[:].bitcast(I32), in_=w1_words[0].bitcast(I32))
         dw_g = tile([P, S], U32, "dw_g", tag="xs")
@@ -90,8 +91,8 @@ def tile_picked_scoretan_none_po_kernel(
         nc.gpsimd.tensor_scalar(above[:], below[:], -1.0, 0.0, ALU.mult, ALU.add)
         rg = tile([P, PACK], F32, "rg", tag="dw")
         nc.vector.reciprocal(rg[:], above[:])
-        w1s = tile([P, S], U8, "w1s", tag="xs")
-        nc.vector.memset(w1s[:].bitcast(I32), 0)
+        w1s = tile([P, S], U8, "w1s", tag="above")
+        nc.gpsimd.memset(w1s[:].bitcast(I32), 0)
         for q in range(4):
             nc.sync.dma_start(out=w1s[32 * q : 32 * q + 4, :].bitcast(I32), in_=w1_scales[0, 4 * q : 4 * q + 4, :].bitcast(I32))
         xw_g = tile([P, S], U32, "xw_g")
@@ -128,9 +129,9 @@ def tile_picked_scoretan_none_po_kernel(
 
         win = [tile([P, S], F32, "win_%d" % t) for t in range(PACK)]
         plain = {(t, 0): tile([P, HALF], F32, "plain_%d" % t)[:] for t in range(PACK)}
-        plain[0, 1] = tile([P, HALF], F32, "plain_0_1")[:]
-        diff = [[tile([P, HALF], F32, "diff_%d_%d" % (t, h)) for h in range(2)] for t in range(PACK)]
-        tanh = [tile([P, S], F32, "tanh_%d" % t) for t in range(PACK)]
+        late = {t: tile([P, HALF], F32, "copied_%d" % t)[:] for t in range(PACK)}
+        diff = {(t, 0): tile([P, HALF], F32, "diff_%d_0" % t)[:] for t in range(PACK)}
+        tanh = {(t, ch): tile([P, n], F32, "tanh_%d_%d" % (t, ch))[:] for ch, (c0, n) in enumerate(CHUNKS) for t in range(PACK)}
         zf = {}
         oq = tile([P, S], U32, "oq")
         osc = tile([P, S], U8, "osc")
@@ -150,20 +151,24 @@ def tile_picked_scoretan_none_po_kernel(
         def own(t, h):
             scaled(plain[t, h], raw_half(t, h), t)
 
+        def own_late(t):
+            plain[t, 1] = late[t]
+            nc.sync.dma_start(out=late[t], in_=win[t][:, half(1)])
+
         def sub(t, h):
-            nc.vector.tensor_tensor(diff[t][h][:], win[t][:].indirect(n2_t[:, 16 * h : 16 * h + 16]), plain[t, h], ALU.subtract)
+            nc.vector.tensor_tensor(diff[t, h], win[t][:].indirect(n2_t[:, 16 * h : 16 * h + 16]), plain[t, h], ALU.subtract)
 
         def th(t, ch):
             c0, n = CHUNKS[ch]
-            src = diff[t][c0 // HALF][:, c0 % HALF : c0 % HALF + n]
-            nc.scalar.activation(tanh[t][:, c0 : c0 + n], src, ACT.Tanh, scale=rg[:, t : t + 1])
+            src = diff[t, c0 // HALF][:, c0 % HALF : c0 % HALF + n]
+            nc.scalar.activation(tanh[t, ch], src, ACT.Tanh, scale=rg[:, t : t + 1])
 
         def mul(t, ch):
             c0, n = CHUNKS[ch]
             if t == 0:
                 zf[ch] = tile([P, PACK, n], F32, "zf_%d" % ch)
             nc.vector.tensor_tensor(
-                zf[ch][:, t, :], win[t][:].indirect(n1_t[:, c0 // 16 : (c0 + n) // 16]), tanh[t][:, c0 : c0 + n], ALU.mult
+                zf[ch][:, t, :], win[t][:].indirect(n1_t[:, c0 // 16 : (c0 + n) // 16]), tanh[t, ch], ALU.mult
             )
 
         def weave_views(dst, src):
@@ -191,7 +196,8 @@ def tile_picked_scoretan_none_po_kernel(
 
         def mm2(ch):
             c0, n = CHUNKS[ch]
-            per = S // n
+            last = ch == len(CHUNKS) - 1
+            per = 2 if last else S // n
             of[ch] = tile([P, PACK, n], F32, "of_%d" % ch)
             for b in range(PACK // per):
                 bank = ps.tile([P, per, n], F32, name="acc_%d_%d" % (ch, b), tag="acc", bufs=3)
@@ -206,7 +212,10 @@ def tile_picked_scoretan_none_po_kernel(
                         start=True,
                         stop=True,
                     )
-                nc.scalar.copy(of[ch][:, b * per : (b + 1) * per, :], bank[:])
+                if last and b == 1:
+                    nc.vector.tensor_copy(of[ch][:, b * per : (b + 1) * per, :], bank[:])
+                else:
+                    nc.scalar.copy(of[ch][:, b * per : (b + 1) * per, :], bank[:])
             nc.sync.dma_start(out=out_0.rearrange("(p t) j -> p t j", t=PACK)[:, :, c0 : c0 + n], in_=of[ch][:])
 
         def weave_o(ch, eng):
@@ -221,32 +230,29 @@ def tile_picked_scoretan_none_po_kernel(
         def quant_o(ch):
             c0, n = CHUNKS[ch]
             nc.vector.quantize_mx(out=oq[:, c0 : c0 + n].bitcast(FP8X4), scales=osc[:, c0 : c0 + n], in_=ob[ch][:])
-            nc.sync.dma_start(
-                out=out_1[0].rearrange("p n t -> p (n t)").bitcast(I32)[:, c0 : c0 + n],
-                in_=oq[:, c0 : c0 + n].bitcast(I32),
-            )
+
 
         scaled(win[0][:, half(0)], raw[0, 0], 0)
-        own(0, 0)
+        nc.vector.tensor_copy(plain[0, 0], win[0][:, half(0)])
         scaled(win[0][:, half(1)], raw[0, 1], 0)
+        own_late(0)
         sub(0, 0)
         for t in range(1, PACK):
             window(t)
+            own_late(t)
             own(t, 0)
             sub(t, 0)
             th(t - 1, 0)
             mul(t - 1, 0)
-            if t == 1:
-                w1s_d = tile([P, S], U8, "w1s_d", tag="diff_0_0")
-                deal(w1s_d[:], w1s[:], 16)
-        own(0, 1)
+        diff[0, 1] = tile([P, HALF], F32, "diff_0_1")[:]
         sub(0, 1)
         th(PACK - 1, 0)
         mul(PACK - 1, 0)
-        late = tile([P, PACK - 1, HALF], F32, "late", tag="diff_3_0")
+        w1s_d = tile([P, S], U8, "w1s_d", tag="diff_3_0")
+        deal(w1s_d[:], w1s[:], 16)
+        rest = tile([P, PACK - 1, HALF], F32, "diff_rest", tag="tanh_3_0")
         for t in range(1, PACK):
-            plain[t, 1] = late[:, t - 1, :]
-            own(t, 1)
+            diff[t, 1] = rest[:, t - 1, :]
             sub(t, 1)
         weave_z(0, "s")
         quant_z(0)
@@ -265,8 +271,12 @@ def tile_picked_scoretan_none_po_kernel(
         weave_o(1, "v")
         quant_o(0)
         quant_o(1)
+        words = out_1[0].rearrange("p n t -> p (n t)").bitcast(I32)
+        cut = CHUNKS[-1][0]
+        nc.sync.dma_start(out=words[:, 0:cut], in_=oq[:, 0:cut].bitcast(I32))
         weave_o(2, "v")
         quant_o(2)
+        nc.scalar.dma_start(out=words[:, cut:S], in_=oq[:, cut:S].bitcast(I32))
         for q in range(4):
-            queue = nc.scalar if q % 2 else nc.sync
+            queue = nc.scalar if q == 3 else nc.sync
             queue.dma_start(out=out_2[0, 4 * q : 4 * q + 4, :].bitcast(I32), in_=osc[32 * q : 32 * q + 4, :].bitcast(I32))

@@ -129,7 +129,7 @@ def tile_picked_scoretan_none_po_kernel(
 
         win = [tile([P, S], F32, "win_%d" % t) for t in range(PACK)]
         plain = {(t, 0): tile([P, HALF], F32, "plain_%d" % t)[:] for t in range(PACK)}
-        late = {t: tile([P, HALF], F32, "copied_%d" % t)[:] for t in range(PACK)}
+        late = {t: tile([P, HALF], F32, "copied_%d" % t)[:] for t in range(1, PACK)}
         diff = {(t, 0): tile([P, HALF], F32, "diff_%d_0" % t)[:] for t in range(PACK)}
         tanh = {(t, ch): tile([P, n], F32, "tanh_%d_%d" % (t, ch))[:] for ch, (c0, n) in enumerate(CHUNKS) for t in range(PACK)}
         zf = {}
@@ -235,8 +235,11 @@ def tile_picked_scoretan_none_po_kernel(
         scaled(win[0][:, half(0)], raw[0, 0], 0)
         nc.vector.tensor_copy(plain[0, 0], win[0][:, half(0)])
         scaled(win[0][:, half(1)], raw[0, 1], 0)
-        own_late(0)
+        plain[0, 1] = tile([P, HALF], F32, "plain_0_1")[:]
+        nc.vector.tensor_copy(plain[0, 1], win[0][:, half(1)])
         sub(0, 0)
+        diff[0, 1] = tile([P, HALF], F32, "diff_0_1")[:]
+        sub(0, 1)
         for t in range(1, PACK):
             window(t)
             own_late(t)
@@ -244,8 +247,6 @@ def tile_picked_scoretan_none_po_kernel(
             sub(t, 0)
             th(t - 1, 0)
             mul(t - 1, 0)
-        diff[0, 1] = tile([P, HALF], F32, "diff_0_1")[:]
-        sub(0, 1)
         th(PACK - 1, 0)
         mul(PACK - 1, 0)
         w1s_d = tile([P, S], U8, "w1s_d", tag="diff_3_0")
@@ -260,16 +261,16 @@ def tile_picked_scoretan_none_po_kernel(
             for t in range(PACK):
                 th(t, ch)
                 mul(t, ch)
-        weave_z(1, "s")
         mm2(0)
+        weave_z(1, "s")
         quant_z(1)
+        weave_o(0, "s")
         mm2(1)
         weave_z(2, "v")
         quant_z(2)
-        mm2(2)
-        weave_o(0, "v")
-        weave_o(1, "v")
         quant_o(0)
+        weave_o(1, "v")
+        mm2(2)
         quant_o(1)
         words = out_1[0].rearrange("p n t -> p (n t)").bitcast(I32)
         cut = CHUNKS[-1][0]

@@ -43,14 +43,11 @@ def tile_picked_scoretan_none_po_kernel(
         xs = tile([P, TABLE], U8, "xs")
 
         nc.gpsimd.memset(xs[:].bitcast(I32), 0)
-        warm = tile([P, 2], F32, "warm")
-        nc.vector.memset(warm[:, 0:1], 0.0)
         gn_t = tile([P, PACK], F32, "gn_t")
 
         nc.sync.dma_start(kidx_t[:], kidx)
         nc.sync.dma_start(out=ds[:].bitcast(I32), in_=d_scales[0].bitcast(I32).unsqueeze(1).to_broadcast([16, 8, TABLE // 4]))
         nc.scalar.dma_start(out=xs[0:P:8, :].bitcast(I32), in_=x_scales[0].bitcast(I32))
-        nc.scalar.activation(warm[:, 1:2], warm[:, 0:1], ACT.Tanh)
         nc.sync.dma_start(offs_t[:], offs)
         nc.sync.dma_start(out=gn_t[:], in_=gn.rearrange("(p t) o -> p (t o)", t=PACK))
         nc.sync.dma_start(n2_t[:], n2)
@@ -81,7 +78,7 @@ def tile_picked_scoretan_none_po_kernel(
         dw_d = tile([P, S], U32, "dw_d")
         deal(dw_d[:].bitcast(I32), dw_g[:].bitcast(I32), 4)
         gs = tile([P, PACK], F32, "gs")
-        nc.gpsimd.tensor_scalar(gs[:], gn_t[:], 0.0625, 0.0, ALU.mult, ALU.add)
+        nc.scalar.activation(gs[:], gn_t[:], ACT.Copy, scale=0.0625)
         above = tile([P, PACK], F32, "above")
         nc.gpsimd.tensor_scalar(above[:], gn_t[:], -TINY, None, ALU.is_gt)
         below = tile([P, PACK], F32, "below")

from contextlib import ExitStack

import concourse.mybir as mybir

F32 = mybir.dt.float32
BF16 = mybir.dt.bfloat16
I32 = mybir.dt.int32
U32 = mybir.dt.uint32
U16 = mybir.dt.uint16
U8 = mybir.dt.uint8
FP8X4 = mybir.dt.float8_e4m3fn_x4
FP4X4 = mybir.dt.float4_e2m1fn_x4
ACT = mybir.ActivationFunctionType
ALU = mybir.AluOpType

P = 128
PACK = 4
TABLE = 2048
S = 512
HALF = 256
CHUNKS = ((0, 256), (256, 128), (384, 128))
TINY = 2.0**-126
FLOPS = 2 * 2 * 512 * 512 * 512


def tile_picked_scoretan_none_po_kernel(
    tc, x_words, x_scales, d_words, d_scales, gn, w1_words, w1_scales, offs, kidx, n1, n2, out_0, out_1, out_2
):
    nc = tc.nc
    with ExitStack() as ctx:
        sb = ctx.enter_context(tc.tile_pool(name="sb", bufs=1))
        ps = ctx.enter_context(tc.psum_pool(name="ps", bufs=1))

        def tile(shape, dtype, name, tag=None):
            return sb.tile(shape, dtype, name=name, tag=tag or name, align_bytes=64)

        kidx_t = tile([P, S // 16], U16, "kidx_t")
        offs_t = tile([P, S // 16], U16, "offs_t")
        n1_t = tile([P, S // 16], U16, "n1_t")
        n2_t = tile([P, S // 16], U16, "n2_t")
        dw = tile([P, TABLE], U32, "dw")
        ds = tile([P, TABLE], U8, "ds")
        xs = tile([P, TABLE], U8, "xs")

        nc.gpsimd.memset(xs[:].bitcast(I32), 0)
        gn_t = tile([P, PACK], F32, "gn_t")

        nc.sync.dma_start(kidx_t[:], kidx)
        nc.sync.dma_start(out=ds[:].bitcast(I32), in_=d_scales[0].bitcast(I32).unsqueeze(1).to_broadcast([16, 8, TABLE // 4]))
        nc.scalar.dma_start(out=xs[0:P:8, :].bitcast(I32), in_=x_scales[0].bitcast(I32))
        nc.sync.dma_start(offs_t[:], offs)
        nc.sync.dma_start(out=gn_t[:], in_=gn.rearrange("(p t) o -> p (t o)", t=PACK))
        nc.sync.dma_start(n2_t[:], n2)
        nc.sync.dma_start(n1_t[:], n1)
        nc.sync.dma_start(out=dw[:].bitcast(I32), in_=d_words[0].rearrange("p n t -> p (n t)").bitcast(I32))
        xw = tile([P, TABLE], U32, "xw")
        nc.sync.dma_start(out=xw[:].bitcast(I32), in_=x_words[0].rearrange("p n t -> p (n t)").bitcast(I32))

        def deal(dst, src, run):
            nc.vector.tensor_copy(
                out=dst.rearrange("p (t c i) -> p c t i", t=PACK, i=run),
                in_=src.rearrange("p (c i t) -> p c t i", t=PACK, i=run),
            )

        ds_g = tile([P, S], U8, "ds_g")
        nc.vector.tensor_copy(ds_g[:], ds[:].indirect(kidx_t[:]))
        xs_g = tile([P, S], U8, "xs_g")
        nc.vector.tensor_copy(xs_g[:], xs[:].indirect(offs_t[:]))
        sc = tile([P, 2 * S], U8, "sc")
        deal(sc[:, 0:S], ds_g[:], 16)
        nc.vector.tensor_copy(sc[:, S : 2 * S].bitcast(I32), xs_g[:].bitcast(I32))
        for r in range(1, 4):
            nc.scalar.dma_start(out=sc[r:P:32, :].bitcast(I32), in_=sc[8 * r : P : 32, :].bitcast(I32))
        w1w = tile([P, 2 * S], U8, "w1w", tag="xs_g")
        nc.scalar.dma_start(out=w1w[:].bitcast(I32), in_=w1_words[0].bitcast(I32))
        dw_g = tile([P, S], U32, "dw_g", tag="xs")
        nc.vector.tensor_copy(dw_g[:], dw[:].indirect(kidx_t[:]))
        dw_d = tile([P, S], U32, "dw_d")
        deal(dw_d[:].bitcast(I32), dw_g[:].bitcast(I32), 4)
        gs = tile([P, PACK], F32, "gs")
        nc.scalar.activation(gs[:], gn_t[:], ACT.Copy, scale=0.0625)
        above = tile([P, PACK], F32, "above")
        nc.gpsimd.tensor_scalar(above[:], gn_t[:], -TINY, None, ALU.is_gt)
        below = tile([P, PACK], F32, "below")
        nc.gpsimd.tensor_scalar(below[:], gn_t[:], TINY, None, ALU.is_lt)
        nc.gpsimd.tensor_tensor(above[:], above[:], below[:], ALU.mult)
        nc.gpsimd.tensor_tensor(below[:], above[:], gn_t[:], ALU.add)
        nc.gpsimd.tensor_scalar(above[:], below[:], -1.0, 0.0, ALU.mult, ALU.add)
        rg = tile([P, PACK], F32, "rg", tag="dw")
        nc.vector.reciprocal(rg[:], above[:])
        w1s = tile([P, S], U8, "w1s", tag="above")
        nc.gpsimd.memset(w1s[:].bitcast(I32), 0)
        for q in range(4):
            nc.sync.dma_start(out=w1s[32 * q : 32 * q + 4, :].bitcast(I32), in_=w1_scales[0, 4 * q : 4 * q + 4, :].bitcast(I32))
        xw_g = tile([P, S], U32, "xw_g")
        for h in range(2):
            nc.vector.tensor_copy(xw_g[:, h * HALF : (h + 1) * HALF], xw[:].indirect(offs_t[:, 16 * h : 16 * h + 16]))

        def mm1(acc, t, c0, n):
            nc.tensor.matmul_mx(
                out=acc,
                lhsT=dw_d[:, t * P : (t + 1) * P].bitcast(FP8X4),
                lhsT_scale=sc[:, t * P : (t + 1) * P],
                rhs=xw_g[:, c0 : c0 + n].bitcast(FP8X4),
                rhs_scale=sc[:, S + c0 : S + c0 + n],
                start=True,
                stop=True,
            )

        raw = {}
        for h in range(2):
            bank = ps.tile([P, HALF], F32, name="raw0%d" % h)
            mm1(bank[:], 0, h * HALF, HALF)
            raw[0, h] = bank[:]
        for t in range(1, PACK):
            bank = ps.tile([P, S], F32, name="raw%d" % t)
            mm1(bank[:], t, 0, S)
            raw[t] = bank

        w1w_d = tile([P, 2 * S], U8, "w1w_d", tag="xw")
        nc.vector.tensor_copy(
            out=w1w_d[:].rearrange("p (t c i b) -> p c t i b", t=PACK, i=8, b=2),
            in_=w1w[:].rearrange("p (c i t b) -> p c t i b", t=PACK, i=8, b=2),
        )


        win = [tile([P, S], F32, "win_%d" % t) for t in range(PACK)]
        plain = {(t, 0): tile([P, HALF], F32, "plain_%d" % t)[:] for t in range(PACK)}
        late = {t: tile([P, HALF], F32, "copied_%d" % t)[:] for t in range(1, PACK)}
        diff = {(t, 0): tile([P, HALF], F32, "diff_%d_0" % t)[:] for t in range(PACK)}
        tanh = {(t, ch): tile([P, n], F32, "tanh_%d_%d" % (t, ch))[:] for ch, (c0, n) in enumerate(CHUNKS) for t in range(PACK)}
        zf = {}
        oq = tile([P, S], U32, "oq")
        osc = tile([P, S], U8, "osc")

        def half(h):
            return slice(h * HALF, (h + 1) * HALF)

        def raw_half(t, h):
            return raw[0, h] if t == 0 else raw[t][:, half(h)]

        def scaled(dst, src, t):
            nc.scalar.activation(dst, src, ACT.Copy, scale=gs[:, t : t + 1])

        def window(t):
            scaled(win[t][:], raw[t][:], t)

        def own(t, h):
            scaled(plain[t, h], raw_half(t, h), t)

        def own_late(t):
            plain[t, 1] = late[t]
            nc.sync.dma_start(out=late[t], in_=win[t][:, half(1)])

        def sub(t, h):
            nc.vector.tensor_tensor(diff[t, h], win[t][:].indirect(n2_t[:, 16 * h : 16 * h + 16]), plain[t, h], ALU.subtract)

        def th(t, ch):
            c0, n = CHUNKS[ch]
            src = diff[t, c0 // HALF][:, c0 % HALF : c0 % HALF + n]
            nc.scalar.activation(tanh[t, ch], src, ACT.Tanh, scale=rg[:, t : t + 1])

        def mul(t, ch):
            c0, n = CHUNKS[ch]
            if t == 0:
                zf[ch] = tile([P, PACK, n], F32, "zf_%d" % ch)
            nc.vector.tensor_tensor(
                zf[ch][:, t, :], win[t][:].indirect(n1_t[:, c0 // 16 : (c0 + n) // 16]), tanh[t, ch], ALU.mult
            )

        def weave_views(dst, src):
            return (
                dst[:].rearrange("p (c i t) -> p c t i", t=PACK, i=4),
                src[:].rearrange("p t (c i) -> p c t i", i=4),
            )

        zb, zq, zs, acc, of, ob = {}, {}, {}, {}, {}, {}

        def weave_z(ch, eng):
            n = CHUNKS[ch][1]
            zb[ch] = tile([P, PACK * n], BF16, "zb_%d" % ch, tag="zb_%d" % min(ch, 1))
            d, s = weave_views(zb[ch], zf[ch])
            if eng == "s":
                nc.scalar.copy(d, s)
            else:
                nc.vector.tensor_copy(d, s)

        def quant_z(ch):
            n = CHUNKS[ch][1]
            zq[ch] = tile([P, n], U32, "zq_%d" % ch)
            zs[ch] = tile([P, n], U8, "zs_%d" % ch)
            nc.vector.quantize_mx(out=zq[ch][:].bitcast(FP8X4), scales=zs[ch][:], in_=zb[ch][:])

        def mm2(ch):
            c0, n = CHUNKS[ch]
            last = ch == len(CHUNKS) - 1
            per = 2 if last else S // n
            of[ch] = tile([P, PACK, n], F32, "of_%d" % ch)
            for b in range(PACK // per):
                bank = ps.tile([P, per, n], F32, name="acc_%d_%d" % (ch, b), tag="acc", bufs=3)
                for u in range(per):
                    t = b * per + u
                    nc.tensor.matmul_mx(
                        out=bank[:, u, :],
                        lhsT=w1w_d[:, 2 * t * P : 2 * (t + 1) * P].bitcast(FP4X4),
                        lhsT_scale=w1s_d[:, t * P : (t + 1) * P],
                        rhs=zq[ch][:].bitcast(FP8X4),
                        rhs_scale=zs[ch][:],
                        start=True,
                        stop=True,
                    )
                if last and b == 1:
                    nc.vector.tensor_copy(of[ch][:, b * per : (b + 1) * per, :], bank[:])
                else:
                    nc.scalar.copy(of[ch][:, b * per : (b + 1) * per, :], bank[:])
            nc.sync.dma_start(out=out_0.rearrange("(p t) j -> p t j", t=PACK)[:, :, c0 : c0 + n], in_=of[ch][:])

        def weave_o(ch, eng):
            n = CHUNKS[ch][1]
            ob[ch] = tile([P, PACK * n], BF16, "ob_%d" % ch)
            d, s = weave_views(ob[ch], of[ch])
            if eng == "s":
                nc.scalar.copy(d, s)
            else:
                nc.vector.tensor_copy(d, s)

        def quant_o(ch):
            c0, n = CHUNKS[ch]
            nc.vector.quantize_mx(out=oq[:, c0 : c0 + n].bitcast(FP8X4), scales=osc[:, c0 : c0 + n], in_=ob[ch][:])


        scaled(win[0][:, half(0)], raw[0, 0], 0)
        nc.vector.tensor_copy(plain[0, 0], win[0][:, half(0)])
        scaled(win[0][:, half(1)], raw[0, 1], 0)
        plain[0, 1] = tile([P, HALF], F32, "plain_0_1")[:]
        nc.vector.tensor_copy(plain[0, 1], win[0][:, half(1)])
        sub(0, 0)
        diff[0, 1] = tile([P, HALF], F32, "diff_0_1")[:]
        sub(0, 1)
        for t in range(1, PACK):
            window(t)
            own_late(t)
            own(t, 0)
            sub(t, 0)
            th(t - 1, 0)
            mul(t - 1, 0)
        th(PACK - 1, 0)
        mul(PACK - 1, 0)
        w1s_d = tile([P, S], U8, "w1s_d", tag="diff_3_0")
        deal(w1s_d[:], w1s[:], 16)
        rest = tile([P, PACK - 1, HALF], F32, "diff_rest", tag="tanh_3_0")
        for t in range(1, PACK):
            diff[t, 1] = rest[:, t - 1, :]
            sub(t, 1)
        weave_z(0, "s")
        quant_z(0)
        for ch in (1, 2):
            for t in range(PACK):
                th(t, ch)
                mul(t, ch)
        mm2(0)
        weave_z(1, "s")
        quant_z(1)
        weave_o(0, "s")
        mm2(1)
        weave_z(2, "v")
        quant_z(2)
        quant_o(0)
        weave_o(1, "v")
        mm2(2)
        quant_o(1)
        words = out_1[0].rearrange("p n t -> p (n t)").bitcast(I32)
        cut = CHUNKS[-1][0]
        nc.sync.dma_start(out=words[:, 0:cut], in_=oq[:, 0:cut].bitcast(I32))
        weave_o(2, "v")
        quant_o(2)
        nc.scalar.dma_start(out=words[:, cut:S], in_=oq[:, cut:S].bitcast(I32))
        for q in range(4):
            queue = nc.scalar if q == 3 else nc.sync
            queue.dma_start(out=out_2[0, 4 * q : 4 * q + 4, :].bitcast(I32), in_=osc[32 * q : 32 * q + 4, :].bitcast(I32))
